import numpy as np
import ml_dtypes

BF16 = ml_dtypes.bfloat16


def bf(x):
    return np.asarray(x, np.float32).astype(BF16)


def f32(x):
    return np.asarray(x, np.float32)


def f64(x):
    return np.asarray(x).astype(np.float64)


def striped(idx):
    return np.tile(idx.reshape(-1, 16).T, (8, 1))


def rows(idx, k):
    return np.tile(idx, (k, 1))


def look(tab, idx):
    return np.take_along_axis(f64(tab), rows(idx, len(tab)), axis=1)


K, S, V, N, M = 512, 2048, 1536, 1536, 512


def setup_inputs():
    return {"tab": f32(np.random.standard_normal((K, S))), "w": bf(np.random.standard_normal((K, M)) / np.sqrt(K)), "b": f32(0.5 * np.random.standard_normal((M, 1))), "offs": striped(np.random.randint(0, S, N))}


def reference(tab, w, b, offs):
    idx = offs[:16].T.reshape(-1)
    t = look(tab, idx)
    x = 0.75 * t + 0.25
    y = f64(w).T @ x
    return y + f64(b)

@@ -1,0 +1,53 @@
+import concourse.mybir as mybir
+
+F32, BF16, U16 = mybir.dt.float32, mybir.dt.bfloat16, mybir.dt.uint16
+MULT, ADD = mybir.AluOpType.mult, mybir.AluOpType.add
+IDENTITY = mybir.ActivationFunctionType.Identity
+
+P = 128
+K, S, N, M = 512, 2048, 1536, 512
+PIECE = 512
+SCALE, SHIFT = 0.75, 0.25
+FLOPS = 2 * K * M * N
+
+
+def tile_lookup_deq_aff_bias_kernel(tc, tab, w, b, offs, out):
+    nc = tc.nc
+    k_blocks, m_blocks, pieces = K // P, M // P, N // PIECE
+    with (
+        tc.tile_pool(name="held", bufs=1) as held,
+        tc.tile_pool(name="results", bufs=pieces) as results,
+        tc.psum_pool(name="psum", bufs=8) as psum,
+    ):
+        offsets = held.tile([P, N // 16], U16, name="offsets")
+        nc.sync.dma_start(offsets[:], offs)
+
+        windows, weights = [], []
+        for k in range(k_blocks):
+            window = held.tile([P, S], F32, name=f"window{k}")
+            nc.sync.dma_start(window[:], tab[k * P : (k + 1) * P, :])
+            weight = held.tile([P, M], BF16, name=f"weight{k}")
+            nc.sync.dma_start(weight[:], w[k * P : (k + 1) * P, :])
+            windows.append(window)
+            weights.append(weight)
+
+        bias = held.tile([P, m_blocks], F32, name="bias")
+        with nc.allow_non_contiguous_dma(reason="one bias value for each partition and block of outputs"):
+            nc.scalar.dma_start(bias[:], b.rearrange("(m p) o -> p (m o)", p=P))
+
+        out_blocks = out.rearrange("(m p) n -> p m n", p=P)
+        for c in range(pieces):
+            sums = [psum.tile([P, PIECE], F32, name="sums") for m in range(m_blocks)]
+            piece_offsets = offsets[:, c * PIECE // 16 : (c + 1) * PIECE // 16]
+            for k in range(k_blocks):
+                x = held.tile([P, PIECE], BF16, name=f"x{c}_{k}")
+                nc.vector.tensor_scalar(x[:], windows[k][:].indirect(piece_offsets), SCALE, SHIFT, MULT, ADD)
+                for m in range(m_blocks):
+                    nc.tensor.matmul(
+                        sums[m][:], weights[k][:, m * P : (m + 1) * P], x[:],
+                        start=(k == 0), stop=(k == k_blocks - 1),
+                    )
+            result = results.tile([P, m_blocks, PIECE], F32, name="result")
+            for m in range(m_blocks):
+                nc.scalar.activation(result[:, m, :], sums[m][:], IDENTITY, bias=bias[:, m : m + 1])
+                nc.sync.dma_start(out_blocks[:, m, c * PIECE : (c + 1) * PIECE], result[:, m, :])

@@ -6,7 +6,8 @@ IDENTITY = mybir.ActivationFunctionType.Identity
 
 P = 128
 K, S, N, M = 512, 2048, 1536, 512
-PIECE = 512
+BANKS, BANK_COLUMNS = 8, 512
+PIECE = 256
 SCALE, SHIFT = 0.75, 0.25
 FLOPS = 2 * K * M * N
 
@@ -14,10 +15,13 @@ FLOPS = 2 * K * M * N
 def tile_lookup_deq_aff_bias_kernel(tc, tab, w, b, offs, out):
     nc = tc.nc
     k_blocks, m_blocks, pieces = K // P, M // P, N // PIECE
+    sums_per_bank = BANK_COLUMNS // PIECE
+    banks_per_piece = m_blocks // sums_per_bank
+    early = range(BANKS // banks_per_piece)
+    late = range(len(early), pieces)
     with (
         tc.tile_pool(name="held", bufs=1) as held,
-        tc.tile_pool(name="results", bufs=pieces) as results,
-        tc.psum_pool(name="psum", bufs=8) as psum,
+        tc.psum_pool(name="psum", bufs=BANKS) as psum,
     ):
         offsets = held.tile([P, N // 16], U16, name="offsets")
         nc.sync.dma_start(offsets[:], offs)
@@ -33,21 +37,62 @@ def tile_lookup_deq_aff_bias_kernel(tc, tab, w, b, offs, out):
 
         bias = held.tile([P, m_blocks], F32, name="bias")
         with nc.allow_non_contiguous_dma(reason="one bias value for each partition and block of outputs"):
-            nc.scalar.dma_start(bias[:], b.rearrange("(m p) o -> p (m o)", p=P))
+            nc.sync.dma_start(bias[:], b.rearrange("(m p) o -> p (m o)", p=P))
 
         out_blocks = out.rearrange("(m p) n -> p m n", p=P)
-        for c in range(pieces):
-            sums = [psum.tile([P, PIECE], F32, name="sums") for m in range(m_blocks)]
-            piece_offsets = offsets[:, c * PIECE // 16 : (c + 1) * PIECE // 16]
-            for k in range(k_blocks):
-                x = held.tile([P, PIECE], BF16, name=f"x{c}_{k}")
-                nc.vector.tensor_scalar(x[:], windows[k][:].indirect(piece_offsets), SCALE, SHIFT, MULT, ADD)
-                for m in range(m_blocks):
-                    nc.tensor.matmul(
-                        sums[m][:], weights[k][:, m * P : (m + 1) * P], x[:],
-                        start=(k == 0), stop=(k == k_blocks - 1),
-                    )
-            result = results.tile([P, m_blocks, PIECE], F32, name="result")
+
+        def new_x(piece, k):
+            return held.tile([P, PIECE], BF16, name=f"x{piece}_{k}")
+
+        def look_up(x, piece, k):
+            entries = offsets[:, piece * PIECE // 16 : (piece + 1) * PIECE // 16]
+            nc.vector.tensor_scalar(x[:], windows[k][:].indirect(entries), SCALE, SHIFT, MULT, ADD)
+
+        def new_banks():
+            return [psum.tile([P, sums_per_bank, PIECE], F32, name="bank") for i in range(banks_per_piece)]
+
+        def multiply(banks, x, k):
             for m in range(m_blocks):
-                nc.scalar.activation(result[:, m, :], sums[m][:], IDENTITY, bias=bias[:, m : m + 1])
-                nc.sync.dma_start(out_blocks[:, m, c * PIECE : (c + 1) * PIECE], result[:, m, :])
+                bank, place = divmod(m, sums_per_bank)
+                nc.tensor.matmul(
+                    banks[bank][:, place, :], weights[k][:, m * P : (m + 1) * P], x[:],
+                    start=(k == 0 and place == 0),
+                    stop=(k == k_blocks - 1 and place == sums_per_bank - 1),
+                )
+
+        def finish(banks, piece, vector_helps):
+            for i, bank in enumerate(banks):
+                result = held.tile([P, sums_per_bank, PIECE], F32, name=f"result{piece}_{i}")
+                first = i * sums_per_bank
+                for place in range(sums_per_bank):
+                    value = bias[:, first + place : first + place + 1]
+                    if vector_helps and i % 2 == 1:
+                        nc.vector.tensor_scalar_add(result[:, place, :], bank[:, place, :], value)
+                    else:
+                        nc.scalar.activation(result[:, place, :], bank[:, place, :], IDENTITY, bias=value)
+                columns = slice(piece * PIECE, (piece + 1) * PIECE)
+                nc.sync.dma_start(out_blocks[:, first : first + sums_per_bank, columns], result[:])
+
+        last_k = k_blocks - 1
+        early_banks = [new_banks() for piece in early]
+        ring = []
+        for k in range(k_blocks):
+            for piece in early:
+                x = new_x(piece, k)
+                look_up(x, piece, k)
+                multiply(early_banks[piece], x, k)
+                if k == last_k:
+                    ring.append(x)
+        for piece in early:
+            finish(early_banks[piece], piece, vector_helps=False)
+
+        late_work = [(piece, k) for piece in late for k in range(k_blocks)]
+        late_x = [new_x(*late_work[0])] + [ring[i % len(ring)] for i in range(len(late_work) - 1)]
+        late_banks = {}
+        for (piece, k), x in zip(late_work, late_x):
+            if k == 0:
+                late_banks[piece] = new_banks()
+            look_up(x, piece, k)
+            multiply(late_banks[piece], x, k)
+        for piece in late:
+            finish(late_banks[piece], piece, vector_helps=True)

@@ -1,4 +1,5 @@
 import concourse.mybir as mybir
+from concourse.masks import make_identity
 
 F32, BF16, U16 = mybir.dt.float32, mybir.dt.bfloat16, mybir.dt.uint16
 MULT, ADD = mybir.AluOpType.mult, mybir.AluOpType.add
@@ -35,9 +36,14 @@ def tile_lookup_deq_aff_bias_kernel(tc, tab, w, b, offs, out):
             windows.append(window)
             weights.append(weight)
 
+        bias_rows = held.tile([m_blocks, P], F32, name="bias_rows")
+        nc.scalar.dma_start(bias_rows[:], b.rearrange("(m p) o -> m (p o)", p=P))
+        identity = held.tile([m_blocks, m_blocks], F32, name="identity")
+        make_identity(nc, identity[:])
+        bias_turned = psum.tile([P, m_blocks], F32, name="bias_turned", tag="bank")
+        nc.tensor.matmul(bias_turned[:], bias_rows[:], identity[:], start=True, stop=True)
         bias = held.tile([P, m_blocks], F32, name="bias")
-        with nc.allow_non_contiguous_dma(reason="one bias value for each partition and block of outputs"):
-            nc.sync.dma_start(bias[:], b.rearrange("(m p) o -> p (m o)", p=P))
+        nc.scalar.copy(bias[:], bias_turned[:])
 
         out_blocks = out.rearrange("(m p) n -> p m n", p=P)
 
@@ -51,13 +57,13 @@ def tile_lookup_deq_aff_bias_kernel(tc, tab, w, b, offs, out):
         def new_banks():
             return [psum.tile([P, sums_per_bank, PIECE], F32, name="bank") for i in range(banks_per_piece)]
 
-        def multiply(banks, x, k):
+        def multiply(banks, x, k, order):
             for m in range(m_blocks):
                 bank, place = divmod(m, sums_per_bank)
                 nc.tensor.matmul(
                     banks[bank][:, place, :], weights[k][:, m * P : (m + 1) * P], x[:],
-                    start=(k == 0 and place == 0),
-                    stop=(k == k_blocks - 1 and place == sums_per_bank - 1),
+                    start=(k == order[0] and place == 0),
+                    stop=(k == order[-1] and place == sums_per_bank - 1),
                 )
 
         def finish(banks, piece, vector_helps):
@@ -80,19 +86,23 @@ def tile_lookup_deq_aff_bias_kernel(tc, tab, w, b, offs, out):
             for piece in early:
                 x = new_x(piece, k)
                 look_up(x, piece, k)
-                multiply(early_banks[piece], x, k)
+                multiply(early_banks[piece], x, k, range(k_blocks))
                 if k == last_k:
                     ring.append(x)
         for piece in early:
             finish(early_banks[piece], piece, vector_helps=False)
 
-        late_work = [(piece, k) for piece in late for k in range(k_blocks)]
-        late_x = [new_x(*late_work[0])] + [ring[i % len(ring)] for i in range(len(late_work) - 1)]
-        late_banks = {}
-        for (piece, k), x in zip(late_work, late_x):
-            if k == 0:
-                late_banks[piece] = new_banks()
-            look_up(x, piece, k)
-            multiply(late_banks[piece], x, k)
+        late_order = [last_k] + list(range(last_k))
+        late_banks, reused = {}, 0
+        for piece in late:
+            late_banks[piece] = new_banks()
+            for k in late_order:
+                if k == last_k or (piece, k) == (late[0], 0):
+                    x = new_x(piece, k)
+                else:
+                    x = ring[reused % len(ring)]
+                    reused += 1
+                look_up(x, piece, k)
+                multiply(late_banks[piece], x, k, late_order)
         for piece in late:
             finish(late_banks[piece], piece, vector_helps=True)

@@ -16,9 +16,8 @@ FLOPS = 2 * K * M * N
 def tile_lookup_deq_aff_bias_kernel(tc, tab, w, b, offs, out):
     nc = tc.nc
     k_blocks, m_blocks, pieces = K // P, M // P, N // PIECE
-    sums_per_bank = BANK_COLUMNS // PIECE
-    banks_per_piece = m_blocks // sums_per_bank
-    early = range(BANKS // banks_per_piece)
+    packed = BANK_COLUMNS // PIECE
+    early = range(BANKS * packed // m_blocks)
     late = range(len(early), pieces)
     with (
         tc.tile_pool(name="held", bufs=1) as held,
@@ -54,10 +53,14 @@ def tile_lookup_deq_aff_bias_kernel(tc, tab, w, b, offs, out):
             entries = offsets[:, piece * PIECE // 16 : (piece + 1) * PIECE // 16]
             nc.vector.tensor_scalar(x[:], windows[k][:].indirect(entries), SCALE, SHIFT, MULT, ADD)
 
-        def new_banks():
-            return [psum.tile([P, sums_per_bank, PIECE], F32, name="bank") for i in range(banks_per_piece)]
+        def new_banks(sums_per_bank):
+            return [
+                psum.tile([P, sums_per_bank, PIECE], F32, name="bank")
+                for i in range(m_blocks // sums_per_bank)
+            ]
 
         def multiply(banks, x, k, order):
+            sums_per_bank = m_blocks // len(banks)
             for m in range(m_blocks):
                 bank, place = divmod(m, sums_per_bank)
                 nc.tensor.matmul(
@@ -67,6 +70,7 @@ def tile_lookup_deq_aff_bias_kernel(tc, tab, w, b, offs, out):
                 )
 
         def finish(banks, piece, vector_helps):
+            sums_per_bank = m_blocks // len(banks)
             for i, bank in enumerate(banks):
                 result = held.tile([P, sums_per_bank, PIECE], F32, name=f"result{piece}_{i}")
                 first = i * sums_per_bank
@@ -80,7 +84,7 @@ def tile_lookup_deq_aff_bias_kernel(tc, tab, w, b, offs, out):
                 nc.sync.dma_start(out_blocks[:, first : first + sums_per_bank, columns], result[:])
 
         last_k = k_blocks - 1
-        early_banks = [new_banks() for piece in early]
+        early_banks = [new_banks(packed) for piece in early]
         ring = []
         for k in range(k_blocks):
             for piece in early:
@@ -95,7 +99,7 @@ def tile_lookup_deq_aff_bias_kernel(tc, tab, w, b, offs, out):
         late_order = [last_k] + list(range(last_k))
         late_banks, reused = {}, 0
         for piece in late:
-            late_banks[piece] = new_banks()
+            late_banks[piece] = new_banks(1 if piece == late[-1] else packed)
             for k in late_order:
                 if k == last_k or (piece, k) == (late[0], 0):
                     x = new_x(piece, k)

import concourse.mybir as mybir
from concourse.masks import make_identity

F32, BF16, U16 = mybir.dt.float32, mybir.dt.bfloat16, mybir.dt.uint16
MULT, ADD = mybir.AluOpType.mult, mybir.AluOpType.add
IDENTITY = mybir.ActivationFunctionType.Identity

P = 128
K, S, N, M = 512, 2048, 1536, 512
BANKS, BANK_COLUMNS = 8, 512
PIECE = 256
SCALE, SHIFT = 0.75, 0.25
FLOPS = 2 * K * M * N


def tile_lookup_deq_aff_bias_kernel(tc, tab, w, b, offs, out):
    nc = tc.nc
    k_blocks, m_blocks, pieces = K // P, M // P, N // PIECE
    packed = BANK_COLUMNS // PIECE
    early = range(BANKS * packed // m_blocks)
    late = range(len(early), pieces)
    with (
        tc.tile_pool(name="held", bufs=1) as held,
        tc.psum_pool(name="psum", bufs=BANKS) as psum,
    ):
        offsets = held.tile([P, N // 16], U16, name="offsets")
        nc.sync.dma_start(offsets[:], offs)

        windows, weights = [], []
        for k in range(k_blocks):
            window = held.tile([P, S], F32, name=f"window{k}")
            nc.sync.dma_start(window[:], tab[k * P : (k + 1) * P, :])
            weight = held.tile([P, M], BF16, name=f"weight{k}")
            nc.sync.dma_start(weight[:], w[k * P : (k + 1) * P, :])
            windows.append(window)
            weights.append(weight)

        bias_rows = held.tile([m_blocks, P], F32, name="bias_rows")
        nc.scalar.dma_start(bias_rows[:], b.rearrange("(m p) o -> m (p o)", p=P))
        identity = held.tile([m_blocks, m_blocks], F32, name="identity")
        make_identity(nc, identity[:])
        bias_turned = psum.tile([P, m_blocks], F32, name="bias_turned", tag="bank")
        nc.tensor.matmul(bias_turned[:], bias_rows[:], identity[:], start=True, stop=True)
        bias = held.tile([P, m_blocks], F32, name="bias")
        nc.scalar.copy(bias[:], bias_turned[:])

        out_blocks = out.rearrange("(m p) n -> p m n", p=P)

        def new_x(piece, k):
            return held.tile([P, PIECE], BF16, name=f"x{piece}_{k}")

        def look_up(x, piece, k):
            entries = offsets[:, piece * PIECE // 16 : (piece + 1) * PIECE // 16]
            nc.vector.tensor_scalar(x[:], windows[k][:].indirect(entries), SCALE, SHIFT, MULT, ADD)

        def new_banks(sums_per_bank):
            return [
                psum.tile([P, sums_per_bank, PIECE], F32, name="bank")
                for i in range(m_blocks // sums_per_bank)
            ]

        def multiply(banks, x, k, order):
            sums_per_bank = m_blocks // len(banks)
            for m in range(m_blocks):
                bank, place = divmod(m, sums_per_bank)
                nc.tensor.matmul(
                    banks[bank][:, place, :], weights[k][:, m * P : (m + 1) * P], x[:],
                    start=(k == order[0] and place == 0),
                    stop=(k == order[-1] and place == sums_per_bank - 1),
                )

        def finish(banks, piece, vector_helps):
            sums_per_bank = m_blocks // len(banks)
            for i, bank in enumerate(banks):
                result = held.tile([P, sums_per_bank, PIECE], F32, name=f"result{piece}_{i}")
                first = i * sums_per_bank
                for place in range(sums_per_bank):
                    value = bias[:, first + place : first + place + 1]
                    if vector_helps and i % 2 == 1:
                        nc.vector.tensor_scalar_add(result[:, place, :], bank[:, place, :], value)
                    else:
                        nc.scalar.activation(result[:, place, :], bank[:, place, :], IDENTITY, bias=value)
                columns = slice(piece * PIECE, (piece + 1) * PIECE)
                nc.sync.dma_start(out_blocks[:, first : first + sums_per_bank, columns], result[:])

        last_k = k_blocks - 1
        early_banks = [new_banks(packed) for piece in early]
        ring = []
        for k in range(k_blocks):
            for piece in early:
                x = new_x(piece, k)
                look_up(x, piece, k)
                multiply(early_banks[piece], x, k, range(k_blocks))
                if k == last_k:
                    ring.append(x)
        for piece in early:
            finish(early_banks[piece], piece, vector_helps=False)

        late_order = [last_k] + list(range(last_k))
        late_banks, reused = {}, 0
        for piece in late:
            late_banks[piece] = new_banks(1 if piece == late[-1] else packed)
            for k in late_order:
                if k == last_k or (piece, k) == (late[0], 0):
                    x = new_x(piece, k)
                else:
                    x = ring[reused % len(ring)]
                    reused += 1
                look_up(x, piece, k)
                multiply(late_banks[piece], x, k, late_order)
        for piece in late:
            finish(late_banks[piece], piece, vector_helps=True)
